import numpy as np, ml_dtypes
CORES = [43,171,299,427]
N = 4
def setup_inputs(rng):
    return {"x": rng.standard_normal((N, 128, 256), dtype=np.float32).astype(ml_dtypes.bfloat16)}
def reference(x):
    g = np.concatenate(list(x), axis=1).astype(np.float32)
    return {"y": np.broadcast_to(g, (N,) + g.shape)}

@@ -1,0 +1,93 @@
+from concourse.bass import DstId, RemoteDMATransfer
+
+W = 256
+H = W // 2
+RELAY_CABLE = 0
+RELAY_SWITCH = 4
+
+SCRATCH = {
+    "gb": ("sbuf", [128, 4 * W], "bfloat16"),
+    "yf": ("sbuf", [128, 4 * W], "float32"),
+}
+SEMAPHORES = ["loaded", "sent", "go", "arr_s", "arr_c", "dg_p", "dg_q", "hin",
+              "cv_o", "cv_s", "cv_c", "cv_p", "cv_q", "st_sync", "st_g"]
+
+
+def rank_program(g, core, T, topo):
+    S = T.sem
+    h = topo.host(core)
+    chip0 = (T.cores[0] % 128) // 8 * 8
+    loc = core % 128
+    hs, hc = h ^ 1, 3 - h
+
+    def dst(d):
+        rid, pid = topo.addr(d, core)
+        return DstId(rid=rid, pnc=pid)
+
+    if T.rank_of(core) is None:
+        if loc == chip0 + RELAY_CABLE:
+            src_rank, to, off, sem = hs, T.cores[hc], 0, S.dg_p
+        elif loc == chip0 + RELAY_SWITCH:
+            src_rank, to, off, sem = hc, T.cores[hs], H, S.dg_q
+        else:
+            return
+        rid, pid = topo.addr(to, core)
+        c0 = W * src_rank + off
+        g.wait_ge(S.hin, 4)
+        g.remote_dma(T.gb[:, c0:c0 + H], T.gb[:, 0:H], sem, S.sent, pid, rid, 0xFF)
+        g.wait_ge(S.sent, 8)
+        return
+
+    r = T.rank_of(core)
+
+    def blk(j):
+        return slice(W * j, W * j + W)
+
+    own = W * r
+    v, q = g.vector, g.sync
+
+    q.dma_start(T.gb[:, blk(r)], T.x[:]).then_inc(S.loaded, 16)
+    g.wait_ge(S.loaded, 16)
+    g.remote_dma_fused([
+        RemoteDMATransfer(dst_ids=[dst(hs * 128 + chip0 + RELAY_CABLE)], dma_engine_mask=0x0F, remote_sem=S.hin,
+                          src=T.gb[:, own:own + H], dst=T.gb[:, 0:H]),
+        RemoteDMATransfer(dst_ids=[dst(hc * 128 + chip0 + RELAY_SWITCH)], dma_engine_mask=0xF0, remote_sem=S.hin,
+                          src=T.gb[:, own + H:own + W], dst=T.gb[:, 0:H]),
+    ], local_sem=S.sent)
+    g.remote_dma_fused([
+        RemoteDMATransfer(dst_ids=[dst(T.cores[hs])], dma_engine_mask=0x0F, remote_sem=S.arr_s,
+                          src=T.gb[:, blk(r)], dst=T.gb[:, blk(r)]),
+        RemoteDMATransfer(dst_ids=[dst(T.cores[hc])], dma_engine_mask=0xF0, remote_sem=S.arr_c,
+                          src=T.gb[:, blk(r)], dst=T.gb[:, blk(r)]),
+    ], local_sem=S.sent)
+    g.sem_inc(S.go, 1)
+
+    d = (r + 2) % 4
+    dp, dq = slice(W * d, W * d + H), slice(W * d + H, W * d + W)
+    v.wait_ge(S.loaded, 16)
+    v.tensor_copy(T.yf[:, blk(r)], T.gb[:, blk(r)]).then_inc(S.cv_o, 1)
+    v.wait_ge(S.arr_s, 4)
+    v.tensor_copy(T.yf[:, blk(hs)], T.gb[:, blk(hs)]).then_inc(S.cv_s, 1)
+    v.wait_ge(S.arr_c, 4)
+    v.tensor_copy(T.yf[:, blk(hc)], T.gb[:, blk(hc)]).then_inc(S.cv_c, 1)
+    v.wait_ge(S.dg_p, 8)
+    v.tensor_copy(T.yf[:, dp], T.gb[:, dp]).then_inc(S.cv_p, 1)
+    v.wait_ge(S.dg_q, 8)
+    v.tensor_copy(T.yf[:, dq], T.gb[:, dq]).then_inc(S.cv_q, 1)
+
+    q.wait_ge(S.go, 1)
+    q.wait_ge(S.cv_o, 1)
+    q.dma_start(T.y[:, blk(r)], T.yf[:, blk(r)]).then_inc(S.st_sync, 16)
+    q.wait_ge(S.cv_s, 1)
+    q.dma_start(T.y[:, blk(hs)], T.yf[:, blk(hs)]).then_inc(S.st_sync, 16)
+    q.wait_ge(S.cv_p, 1)
+    q.dma_start(T.y[:, dp], T.yf[:, dp]).then_inc(S.st_sync, 16)
+
+    g.wait_ge(S.cv_c, 1)
+    g.dma_start(T.y[:, blk(hc)], T.yf[:, blk(hc)]).then_inc(S.st_g, 16)
+    g.wait_ge(S.cv_q, 1)
+    g.dma_start(T.y[:, dq], T.yf[:, dq]).then_inc(S.st_g, 16)
+
+    g.wait_ge(S.sent, 16)
+    g.wait_ge(S.st_g, 32)
+    g.wait_ge(S.st_sync, 48)

@@ -7,10 +7,8 @@ RELAY_SWITCH = 4
 
 SCRATCH = {
     "gb": ("sbuf", [128, 4 * W], "bfloat16"),
-    "yf": ("sbuf", [128, 4 * W], "float32"),
 }
-SEMAPHORES = ["loaded", "sent", "go", "arr_s", "arr_c", "dg_p", "dg_q", "hin",
-              "cv_o", "cv_s", "cv_c", "cv_p", "cv_q", "st_sync", "st_g"]
+SEMAPHORES = ["loaded", "sent", "arr_s", "arr_c", "dg_p", "dg_q", "hin", "st_g"]
 
 
 def rank_program(g, core, T, topo):
@@ -44,9 +42,8 @@ def rank_program(g, core, T, topo):
         return slice(W * j, W * j + W)
 
     own = W * r
-    v, q = g.vector, g.sync
 
-    q.dma_start(T.gb[:, blk(r)], T.x[:]).then_inc(S.loaded, 16)
+    g.sync.dma_start(T.gb[:, blk(r)], T.x[:]).then_inc(S.loaded, 16)
     g.wait_ge(S.loaded, 16)
     g.remote_dma_fused([
         RemoteDMATransfer(dst_ids=[dst(hs * 128 + chip0 + RELAY_CABLE)], dma_engine_mask=0x0F, remote_sem=S.hin,
@@ -60,34 +57,16 @@ def rank_program(g, core, T, topo):
         RemoteDMATransfer(dst_ids=[dst(T.cores[hc])], dma_engine_mask=0xF0, remote_sem=S.arr_c,
                           src=T.gb[:, blk(r)], dst=T.gb[:, blk(r)]),
     ], local_sem=S.sent)
-    g.sem_inc(S.go, 1)
 
     d = (r + 2) % 4
-    dp, dq = slice(W * d, W * d + H), slice(W * d + H, W * d + W)
-    v.wait_ge(S.loaded, 16)
-    v.tensor_copy(T.yf[:, blk(r)], T.gb[:, blk(r)]).then_inc(S.cv_o, 1)
-    v.wait_ge(S.arr_s, 4)
-    v.tensor_copy(T.yf[:, blk(hs)], T.gb[:, blk(hs)]).then_inc(S.cv_s, 1)
-    v.wait_ge(S.arr_c, 4)
-    v.tensor_copy(T.yf[:, blk(hc)], T.gb[:, blk(hc)]).then_inc(S.cv_c, 1)
-    v.wait_ge(S.dg_p, 8)
-    v.tensor_copy(T.yf[:, dp], T.gb[:, dp]).then_inc(S.cv_p, 1)
-    v.wait_ge(S.dg_q, 8)
-    v.tensor_copy(T.yf[:, dq], T.gb[:, dq]).then_inc(S.cv_q, 1)
-
-    q.wait_ge(S.go, 1)
-    q.wait_ge(S.cv_o, 1)
-    q.dma_start(T.y[:, blk(r)], T.yf[:, blk(r)]).then_inc(S.st_sync, 16)
-    q.wait_ge(S.cv_s, 1)
-    q.dma_start(T.y[:, blk(hs)], T.yf[:, blk(hs)]).then_inc(S.st_sync, 16)
-    q.wait_ge(S.cv_p, 1)
-    q.dma_start(T.y[:, dp], T.yf[:, dp]).then_inc(S.st_sync, 16)
-
-    g.wait_ge(S.cv_c, 1)
-    g.dma_start(T.y[:, blk(hc)], T.yf[:, blk(hc)]).then_inc(S.st_g, 16)
-    g.wait_ge(S.cv_q, 1)
-    g.dma_start(T.y[:, dq], T.yf[:, dq]).then_inc(S.st_g, 16)
+    g.dma_start(T.y[:, blk(r)], T.gb[:, blk(r)]).then_inc(S.st_g, 16)
+    g.wait_ge(S.arr_s, 4)
+    g.dma_start(T.y[:, blk(hs)], T.gb[:, blk(hs)]).then_inc(S.st_g, 16)
+    g.wait_ge(S.arr_c, 4)
+    g.dma_start(T.y[:, blk(hc)], T.gb[:, blk(hc)]).then_inc(S.st_g, 16)
+    g.wait_ge(S.dg_p, 8)
+    g.wait_ge(S.dg_q, 8)
+    g.dma_start(T.y[:, blk(d)], T.gb[:, blk(d)]).then_inc(S.st_g, 16)
 
     g.wait_ge(S.sent, 16)
-    g.wait_ge(S.st_g, 32)
-    g.wait_ge(S.st_sync, 48)
+    g.wait_ge(S.st_g, 64)

@@ -1,12 +1,11 @@
 from concourse.bass import DstId, RemoteDMATransfer
 
 W = 256
-H = W // 2
 RELAY_CABLE = 0
 RELAY_SWITCH = 4
 
 SCRATCH = {
-    "gb": ("sbuf", [128, 4 * W], "bfloat16"),
+    "gd": ("dram", [8, 128, 128], "bfloat16"),
 }
 SEMAPHORES = ["loaded", "sent", "arr_s", "arr_c", "dg_p", "dg_q", "hin", "st_g"]
 
@@ -24,15 +23,14 @@ def rank_program(g, core, T, topo):
 
     if T.rank_of(core) is None:
         if loc == chip0 + RELAY_CABLE:
-            src_rank, to, off, sem = hs, T.cores[hc], 0, S.dg_p
+            slot, to, sem = 2 * hs, T.cores[hc], S.dg_p
         elif loc == chip0 + RELAY_SWITCH:
-            src_rank, to, off, sem = hc, T.cores[hs], H, S.dg_q
+            slot, to, sem = 2 * hc + 1, T.cores[hs], S.dg_q
         else:
             return
         rid, pid = topo.addr(to, core)
-        c0 = W * src_rank + off
         g.wait_ge(S.hin, 4)
-        g.remote_dma(T.gb[:, c0:c0 + H], T.gb[:, 0:H], sem, S.sent, pid, rid, 0xFF)
+        g.remote_dma(T.gd[slot], T.gd[0], sem, S.sent, pid, rid, 0xFF)
         g.wait_ge(S.sent, 8)
         return
 
@@ -41,32 +39,36 @@ def rank_program(g, core, T, topo):
     def blk(j):
         return slice(W * j, W * j + W)
 
-    own = W * r
+    p, q = 2 * r, 2 * r + 1
 
-    g.sync.dma_start(T.gb[:, blk(r)], T.x[:]).then_inc(S.loaded, 16)
+    g.sync.dma_start(T.gd[p:p + 2], T.x[:]).then_inc(S.loaded, 16)
     g.wait_ge(S.loaded, 16)
     g.remote_dma_fused([
         RemoteDMATransfer(dst_ids=[dst(hs * 128 + chip0 + RELAY_CABLE)], dma_engine_mask=0x0F, remote_sem=S.hin,
-                          src=T.gb[:, own:own + H], dst=T.gb[:, 0:H]),
+                          src=T.gd[p], dst=T.gd[0]),
         RemoteDMATransfer(dst_ids=[dst(hc * 128 + chip0 + RELAY_SWITCH)], dma_engine_mask=0xF0, remote_sem=S.hin,
-                          src=T.gb[:, own + H:own + W], dst=T.gb[:, 0:H]),
+                          src=T.gd[q], dst=T.gd[0]),
     ], local_sem=S.sent)
     g.remote_dma_fused([
-        RemoteDMATransfer(dst_ids=[dst(T.cores[hs])], dma_engine_mask=0x0F, remote_sem=S.arr_s,
-                          src=T.gb[:, blk(r)], dst=T.gb[:, blk(r)]),
-        RemoteDMATransfer(dst_ids=[dst(T.cores[hc])], dma_engine_mask=0xF0, remote_sem=S.arr_c,
-                          src=T.gb[:, blk(r)], dst=T.gb[:, blk(r)]),
+        RemoteDMATransfer(dst_ids=[dst(T.cores[hs])], dma_engine_mask=0x03, remote_sem=S.arr_s,
+                          src=T.gd[p], dst=T.gd[p]),
+        RemoteDMATransfer(dst_ids=[dst(T.cores[hs])], dma_engine_mask=0x0C, remote_sem=S.arr_s,
+                          src=T.gd[q], dst=T.gd[q]),
+        RemoteDMATransfer(dst_ids=[dst(T.cores[hc])], dma_engine_mask=0x30, remote_sem=S.arr_c,
+                          src=T.gd[p], dst=T.gd[p]),
+        RemoteDMATransfer(dst_ids=[dst(T.cores[hc])], dma_engine_mask=0xC0, remote_sem=S.arr_c,
+                          src=T.gd[q], dst=T.gd[q]),
     ], local_sem=S.sent)
 
     d = (r + 2) % 4
-    g.dma_start(T.y[:, blk(r)], T.gb[:, blk(r)]).then_inc(S.st_g, 16)
+    g.dma_start(T.y[:, blk(r)], T.x[:]).then_inc(S.st_g, 16)
     g.wait_ge(S.arr_s, 4)
-    g.dma_start(T.y[:, blk(hs)], T.gb[:, blk(hs)]).then_inc(S.st_g, 16)
+    g.dma_start(T.y[:, blk(hs)], T.gd[2 * hs:2 * hs + 2]).then_inc(S.st_g, 16)
     g.wait_ge(S.arr_c, 4)
-    g.dma_start(T.y[:, blk(hc)], T.gb[:, blk(hc)]).then_inc(S.st_g, 16)
+    g.dma_start(T.y[:, blk(hc)], T.gd[2 * hc:2 * hc + 2]).then_inc(S.st_g, 16)
     g.wait_ge(S.dg_p, 8)
     g.wait_ge(S.dg_q, 8)
-    g.dma_start(T.y[:, blk(d)], T.gb[:, blk(d)]).then_inc(S.st_g, 16)
+    g.dma_start(T.y[:, blk(d)], T.gd[2 * d:2 * d + 2]).then_inc(S.st_g, 16)
 
     g.wait_ge(S.sent, 16)
     g.wait_ge(S.st_g, 64)

@@ -1,8 +1,7 @@
 from concourse.bass import DstId, RemoteDMATransfer
 
 W = 256
-RELAY_CABLE = 0
-RELAY_SWITCH = 4
+RELAYS = (0, 4)
 
 SCRATCH = {
     "gd": ("dram", [8, 128, 128], "bfloat16"),
@@ -22,16 +21,12 @@ def rank_program(g, core, T, topo):
         return DstId(rid=rid, pnc=pid)
 
     if T.rank_of(core) is None:
-        if loc == chip0 + RELAY_CABLE:
-            slot, to, sem = 2 * hs, T.cores[hc], S.dg_p
-        elif loc == chip0 + RELAY_SWITCH:
-            slot, to, sem = 2 * hc + 1, T.cores[hs], S.dg_q
-        else:
-            return
-        rid, pid = topo.addr(to, core)
-        g.wait_ge(S.hin, 4)
-        g.remote_dma(T.gd[slot], T.gd[0], sem, S.sent, pid, rid, 0xFF)
-        g.wait_ge(S.sent, 8)
+        for k in (0, 1):
+            if loc == chip0 + RELAYS[k]:
+                rid, pid = topo.addr(T.cores[hc], core)
+                g.wait_ge(S.hin, 4)
+                g.remote_dma(T.gd[2 * hs + k], T.gd[0], (S.dg_p, S.dg_q)[k], S.sent, pid, rid, 0xFF)
+                g.wait_ge(S.sent, 8)
         return
 
     r = T.rank_of(core)
@@ -44,19 +39,19 @@ def rank_program(g, core, T, topo):
     g.sync.dma_start(T.gd[p:p + 2], T.x[:]).then_inc(S.loaded, 16)
     g.wait_ge(S.loaded, 16)
     g.remote_dma_fused([
-        RemoteDMATransfer(dst_ids=[dst(hs * 128 + chip0 + RELAY_CABLE)], dma_engine_mask=0x0F, remote_sem=S.hin,
+        RemoteDMATransfer(dst_ids=[dst(hs * 128 + chip0 + RELAYS[0])], dma_engine_mask=0x0F, remote_sem=S.hin,
                           src=T.gd[p], dst=T.gd[0]),
-        RemoteDMATransfer(dst_ids=[dst(hc * 128 + chip0 + RELAY_SWITCH)], dma_engine_mask=0xF0, remote_sem=S.hin,
+        RemoteDMATransfer(dst_ids=[dst(hs * 128 + chip0 + RELAYS[1])], dma_engine_mask=0xF0, remote_sem=S.hin,
                           src=T.gd[q], dst=T.gd[0]),
     ], local_sem=S.sent)
     g.remote_dma_fused([
-        RemoteDMATransfer(dst_ids=[dst(T.cores[hs])], dma_engine_mask=0x03, remote_sem=S.arr_s,
+        RemoteDMATransfer(dst_ids=[dst(T.cores[hc])], dma_engine_mask=0x03, remote_sem=S.arr_c,
                           src=T.gd[p], dst=T.gd[p]),
         RemoteDMATransfer(dst_ids=[dst(T.cores[hs])], dma_engine_mask=0x0C, remote_sem=S.arr_s,
-                          src=T.gd[q], dst=T.gd[q]),
-        RemoteDMATransfer(dst_ids=[dst(T.cores[hc])], dma_engine_mask=0x30, remote_sem=S.arr_c,
                           src=T.gd[p], dst=T.gd[p]),
-        RemoteDMATransfer(dst_ids=[dst(T.cores[hc])], dma_engine_mask=0xC0, remote_sem=S.arr_c,
+        RemoteDMATransfer(dst_ids=[dst(T.cores[hc])], dma_engine_mask=0x30, remote_sem=S.arr_c,
+                          src=T.gd[q], dst=T.gd[q]),
+        RemoteDMATransfer(dst_ids=[dst(T.cores[hs])], dma_engine_mask=0xC0, remote_sem=S.arr_s,
                           src=T.gd[q], dst=T.gd[q]),
     ], local_sem=S.sent)
 

@@ -2,11 +2,12 @@ from concourse.bass import DstId, RemoteDMATransfer
 
 W = 256
 RELAYS = (0, 4)
+HELPER = 6
 
 SCRATCH = {
     "gd": ("dram", [8, 128, 128], "bfloat16"),
 }
-SEMAPHORES = ["loaded", "sent", "arr_s", "arr_c", "dg_p", "dg_q", "hin", "st_g"]
+SEMAPHORES = ["loaded", "sent", "arr_s", "arr_c", "arr_h", "dg_p", "dg_q", "hin", "st_g"]
 
 
 def rank_program(g, core, T, topo):
@@ -21,12 +22,16 @@ def rank_program(g, core, T, topo):
         return DstId(rid=rid, pnc=pid)
 
     if T.rank_of(core) is None:
+        rid, pid = topo.addr(T.cores[hc], core)
         for k in (0, 1):
             if loc == chip0 + RELAYS[k]:
-                rid, pid = topo.addr(T.cores[hc], core)
                 g.wait_ge(S.hin, 4)
                 g.remote_dma(T.gd[2 * hs + k], T.gd[0], (S.dg_p, S.dg_q)[k], S.sent, pid, rid, 0xFF)
                 g.wait_ge(S.sent, 8)
+        if loc == chip0 + HELPER:
+            g.wait_ge(S.hin, 8)
+            g.remote_dma(T.gd[2 * h + 1], T.gd[0], S.arr_h, S.sent, pid, rid, 0xFF)
+            g.wait_ge(S.sent, 8)
         return
 
     r = T.rank_of(core)
@@ -39,18 +44,18 @@ def rank_program(g, core, T, topo):
     g.sync.dma_start(T.gd[p:p + 2], T.x[:]).then_inc(S.loaded, 16)
     g.wait_ge(S.loaded, 16)
     g.remote_dma_fused([
-        RemoteDMATransfer(dst_ids=[dst(hs * 128 + chip0 + RELAYS[0])], dma_engine_mask=0x0F, remote_sem=S.hin,
+        RemoteDMATransfer(dst_ids=[dst(hs * 128 + chip0 + RELAYS[0])], dma_engine_mask=0x000F, remote_sem=S.hin,
                           src=T.gd[p], dst=T.gd[0]),
-        RemoteDMATransfer(dst_ids=[dst(hs * 128 + chip0 + RELAYS[1])], dma_engine_mask=0xF0, remote_sem=S.hin,
+        RemoteDMATransfer(dst_ids=[dst(hs * 128 + chip0 + RELAYS[1])], dma_engine_mask=0x00F0, remote_sem=S.hin,
+                          src=T.gd[q], dst=T.gd[0]),
+        RemoteDMATransfer(dst_ids=[dst(h * 128 + chip0 + HELPER)], dma_engine_mask=0xFF00, remote_sem=S.hin,
                           src=T.gd[q], dst=T.gd[0]),
     ], local_sem=S.sent)
     g.remote_dma_fused([
-        RemoteDMATransfer(dst_ids=[dst(T.cores[hc])], dma_engine_mask=0x03, remote_sem=S.arr_c,
+        RemoteDMATransfer(dst_ids=[dst(T.cores[hc])], dma_engine_mask=0x0F, remote_sem=S.arr_c,
                           src=T.gd[p], dst=T.gd[p]),
-        RemoteDMATransfer(dst_ids=[dst(T.cores[hs])], dma_engine_mask=0x0C, remote_sem=S.arr_s,
+        RemoteDMATransfer(dst_ids=[dst(T.cores[hs])], dma_engine_mask=0x30, remote_sem=S.arr_s,
                           src=T.gd[p], dst=T.gd[p]),
-        RemoteDMATransfer(dst_ids=[dst(T.cores[hc])], dma_engine_mask=0x30, remote_sem=S.arr_c,
-                          src=T.gd[q], dst=T.gd[q]),
         RemoteDMATransfer(dst_ids=[dst(T.cores[hs])], dma_engine_mask=0xC0, remote_sem=S.arr_s,
                           src=T.gd[q], dst=T.gd[q]),
     ], local_sem=S.sent)
@@ -60,10 +65,12 @@ def rank_program(g, core, T, topo):
     g.wait_ge(S.arr_s, 4)
     g.dma_start(T.y[:, blk(hs)], T.gd[2 * hs:2 * hs + 2]).then_inc(S.st_g, 16)
     g.wait_ge(S.arr_c, 4)
-    g.dma_start(T.y[:, blk(hc)], T.gd[2 * hc:2 * hc + 2]).then_inc(S.st_g, 16)
+    g.dma_start(T.y[0:64, blk(hc)], T.gd[2 * hc]).then_inc(S.st_g, 16)
+    g.wait_ge(S.arr_h, 8)
+    g.dma_start(T.y[64:128, blk(hc)], T.gd[2 * hc + 1]).then_inc(S.st_g, 16)
     g.wait_ge(S.dg_p, 8)
     g.wait_ge(S.dg_q, 8)
     g.dma_start(T.y[:, blk(d)], T.gd[2 * d:2 * d + 2]).then_inc(S.st_g, 16)
 
-    g.wait_ge(S.sent, 16)
-    g.wait_ge(S.st_g, 64)
+    g.wait_ge(S.sent, 24)
+    g.wait_ge(S.st_g, 80)

from concourse.bass import DstId, RemoteDMATransfer

W = 256
RELAYS = (0, 4)
HELPER = 6

SCRATCH = {
    "gd": ("dram", [8, 128, 128], "bfloat16"),
}
SEMAPHORES = ["loaded", "sent", "arr_s", "arr_c", "arr_h", "dg_p", "dg_q", "hin", "st_g"]


def rank_program(g, core, T, topo):
    S = T.sem
    h = topo.host(core)
    chip0 = (T.cores[0] % 128) // 8 * 8
    loc = core % 128
    hs, hc = h ^ 1, 3 - h

    def dst(d):
        rid, pid = topo.addr(d, core)
        return DstId(rid=rid, pnc=pid)

    if T.rank_of(core) is None:
        rid, pid = topo.addr(T.cores[hc], core)
        for k in (0, 1):
            if loc == chip0 + RELAYS[k]:
                g.wait_ge(S.hin, 4)
                g.remote_dma(T.gd[2 * hs + k], T.gd[0], (S.dg_p, S.dg_q)[k], S.sent, pid, rid, 0xFF)
                g.wait_ge(S.sent, 8)
        if loc == chip0 + HELPER:
            g.wait_ge(S.hin, 8)
            g.remote_dma(T.gd[2 * h + 1], T.gd[0], S.arr_h, S.sent, pid, rid, 0xFF)
            g.wait_ge(S.sent, 8)
        return

    r = T.rank_of(core)

    def blk(j):
        return slice(W * j, W * j + W)

    p, q = 2 * r, 2 * r + 1

    g.sync.dma_start(T.gd[p:p + 2], T.x[:]).then_inc(S.loaded, 16)
    g.wait_ge(S.loaded, 16)
    g.remote_dma_fused([
        RemoteDMATransfer(dst_ids=[dst(hs * 128 + chip0 + RELAYS[0])], dma_engine_mask=0x000F, remote_sem=S.hin,
                          src=T.gd[p], dst=T.gd[0]),
        RemoteDMATransfer(dst_ids=[dst(hs * 128 + chip0 + RELAYS[1])], dma_engine_mask=0x00F0, remote_sem=S.hin,
                          src=T.gd[q], dst=T.gd[0]),
        RemoteDMATransfer(dst_ids=[dst(h * 128 + chip0 + HELPER)], dma_engine_mask=0xFF00, remote_sem=S.hin,
                          src=T.gd[q], dst=T.gd[0]),
    ], local_sem=S.sent)
    g.remote_dma_fused([
        RemoteDMATransfer(dst_ids=[dst(T.cores[hc])], dma_engine_mask=0x0F, remote_sem=S.arr_c,
                          src=T.gd[p], dst=T.gd[p]),
        RemoteDMATransfer(dst_ids=[dst(T.cores[hs])], dma_engine_mask=0x30, remote_sem=S.arr_s,
                          src=T.gd[p], dst=T.gd[p]),
        RemoteDMATransfer(dst_ids=[dst(T.cores[hs])], dma_engine_mask=0xC0, remote_sem=S.arr_s,
                          src=T.gd[q], dst=T.gd[q]),
    ], local_sem=S.sent)

    d = (r + 2) % 4
    g.dma_start(T.y[:, blk(r)], T.x[:]).then_inc(S.st_g, 16)
    g.wait_ge(S.arr_s, 4)
    g.dma_start(T.y[:, blk(hs)], T.gd[2 * hs:2 * hs + 2]).then_inc(S.st_g, 16)
    g.wait_ge(S.arr_c, 4)
    g.dma_start(T.y[0:64, blk(hc)], T.gd[2 * hc]).then_inc(S.st_g, 16)
    g.wait_ge(S.arr_h, 8)
    g.dma_start(T.y[64:128, blk(hc)], T.gd[2 * hc + 1]).then_inc(S.st_g, 16)
    g.wait_ge(S.dg_p, 8)
    g.wait_ge(S.dg_q, 8)
    g.dma_start(T.y[:, blk(d)], T.gd[2 * d:2 * d + 2]).then_inc(S.st_g, 16)

    g.wait_ge(S.sent, 24)
    g.wait_ge(S.st_g, 80)
